import numpy as np
import ml_dtypes


def mxq(x, axis, fmt="e4m3"):
    dtype, down = {"e4m3": (ml_dtypes.float8_e4m3fn, 7), "e5m2": (ml_dtypes.float8_e5m2, 14)}[fmt]
    v = np.moveaxis(np.asarray(x, np.float32).astype(ml_dtypes.bfloat16).astype(np.float64), axis, -1)
    blocks = v.reshape(v.shape[:-1] + (-1, 32))
    amax = np.abs(blocks).max(-1, keepdims=True)
    byte = np.maximum(np.where(amax > 0, np.frexp(amax)[1] - 1 + 127, 0) - down, 1)
    scale = np.exp2(byte - 127.0)
    codes = (blocks / scale).astype(np.float32).astype(dtype).astype(np.float64)
    return np.moveaxis((codes * scale).reshape(v.shape), -1, axis)


WIDE = False


def mx_kscale(k):
    if not WIDE:
        return np.ones(k)
    levels = np.array([30, -30])
    if k % 512:
        return np.exp2(np.random.permutation(np.resize(levels, k // 32))).repeat(32)
    a = np.empty((k // 512, 16))
    for p in range(k // 512):
        a[p, :8] = np.random.permutation(np.resize(levels, 8))
        for g in range(8):
            far = levels[np.abs(levels - a[p, g]) >= 10]
            a[p, g + 8] = far[np.random.randint(len(far))]
    return np.exp2(a.ravel()).repeat(32)


def f64(x):
    return np.asarray(x).astype(np.float64)


def striped(idx):
    return np.tile(np.asarray(idx).reshape(-1, 16).T, (8, 1)).astype(np.uint16)


def unstriped(offs):
    return offs[:16].T.reshape(-1).astype(np.int64)


E2M1 = np.array([0.0, 0.5, 1.0, 1.5, 2.0, 3.0, 4.0, 6.0, -0.0, -0.5, -1.0, -1.5, -2.0, -3.0, -4.0, -6.0])


def pack_weight(w, fmt):
    k, n = w.shape
    w = f64(np.asarray(w, np.float32).astype(ml_dtypes.bfloat16)).reshape(k // 32, 32, n)
    amax = np.abs(w).max(1)
    if fmt in ("e4m3", "e5m2"):
        byte = np.frexp(amax)[1] - 1 + 127 - (7 if fmt == "e4m3" else 14)
    else:
        mant, ex = np.frexp(amax / 6.0)
        byte = np.where(mant > 0.5, ex, ex - 1) + 127
    byte = np.clip(np.where(amax > 0, byte, 1), 1, 254)
    scaled = (w * np.exp2(127.0 - byte)[:, None, :]).reshape(k, n).astype(np.float32)
    by_word = np.ascontiguousarray(scaled.reshape(k // 512, 128, 4, n).transpose(0, 1, 3, 2))
    if fmt in ("e4m3", "e5m2"):
        words = by_word.astype(ml_dtypes.float8_e4m3fn if fmt == "e4m3" else ml_dtypes.float8_e5m2).view(np.uint8)
    else:
        c = by_word.astype(ml_dtypes.float4_e2m1fn).view(np.uint8) & 0xF
        words = (c[..., 0::2] | (c[..., 1::2] << 4)).reshape(k // 512, 128, 2 * n)
    return np.ascontiguousarray(words), np.ascontiguousarray(byte.astype(np.uint8).reshape(k // 512, 16, n))


def unpack_weight(words, scales, fmt):
    g, _, n = scales.shape
    words = np.ascontiguousarray(words).reshape(g, 128, n, -1)
    if fmt in ("e4m3", "e5m2"):
        vals = words.view(ml_dtypes.float8_e4m3fn if fmt == "e4m3" else ml_dtypes.float8_e5m2).astype(np.float64)
    else:
        nib = np.empty((g, 128, n, 4), np.uint8)
        nib[..., 0::2] = words & 0xF
        nib[..., 1::2] = words >> 4
        vals = E2M1[nib]
    vals = vals * np.repeat(np.exp2(scales.astype(np.float64) - 127.0), 8, axis=1)[..., None]
    return vals.transpose(0, 1, 3, 2).reshape(g * 512, n)


K, T, J, I, V, L = 1024, 1024, 256, 256, 1024, 512


def setup_inputs():
    n = np.random.standard_normal
    idx = np.random.permutation(T)[:J]
    idx2 = np.random.permutation(V)[:I]
    fk = mx_kscale(K)
    fl = mx_kscale(L)
    kyp = pack_weight(n((K, V)) / fk[:, None], "e5m2")
    cxp = pack_weight(n((L, J)) / fl[:, None], "e2m1")
    wcp = pack_weight(n((L, I)) * 1 / np.sqrt(L) * fl[:, None], "e4m3")
    return {
        "xf": (n((K, T)) * 0.03).astype(np.float32),
        "fk": (np.random.uniform(0.5, 2.0, (K, 1)) * fk[:, None]).astype(np.float32),
        "ky_words": kyp[0],
        "ky_scales": kyp[1],
        "bi": (np.random.uniform(-0.7, 0.7, (1, I))).astype(np.float32),
        "cx_words": cxp[0],
        "cx_scales": cxp[1],
        "wc_words": wcp[0],
        "wc_scales": wcp[1],
        "offs": striped(idx),
        "offs2": striped(idx2),
    }


def reference(xf, fk, ky_words, ky_scales, bi, cx_words, cx_scales, wc_words, wc_scales, offs, offs2):
    idx = unstriped(offs)
    idx2 = unstriped(offs2)
    kyu = unpack_weight(ky_words, ky_scales, "e5m2")
    cxu = unpack_weight(cx_words, cx_scales, "e2m1")
    wcu = unpack_weight(wc_words, wc_scales, "e4m3")
    xg = f64(xf)[:, idx]
    x1 = np.pad(xg, ((0, 0), (1, 0)))[:, :J]
    u = (xg - 0.6 * x1) * f64(fk)
    uq = mxq(u, 0, "e5m2")
    kyidx2g = kyu[:, idx2]
    a0 = uq.T @ kyidx2g
    a = a0 + f64(bi)
    q = cxu.T @ wcu
    y = np.maximum(a, q) - 0.5 * np.minimum(a, q)
    return y

@@ -1,0 +1,185 @@
+from contextlib import ExitStack
+
+import concourse.mybir as mybir
+from concourse.masks import make_identity
+
+K, T, J, I, V, L = 1024, 1024, 256, 256, 1024, 512
+FLOPS = 2 * J * I * (K + L)
+
+F32 = mybir.dt.float32
+BF16 = mybir.dt.bfloat16
+I32 = mybir.dt.int32
+U32 = mybir.dt.uint32
+U16 = mybir.dt.uint16
+U8 = mybir.dt.uint8
+E5M2X4 = mybir.dt.float8_e5m2_x4
+E4M3X4 = mybir.dt.float8_e4m3fn_x4
+E2M1X4 = mybir.dt.float4_e2m1fn_x4
+ALU = mybir.AluOpType
+COPY = mybir.ActivationFunctionType.Copy
+
+P = 128
+PACK = 4
+PASSES = K // (P * PACK)
+PLANES = PASSES * PACK
+PAD = 8
+ROW_TILES = J // P
+XF_LOADS = [(0, 2), (2, 2), (4, 1), (5, 1), (6, 1), (7, 1)]
+
+
+def tile_list_scores_steps_listed_tworank_kernel(
+    tc, xf, fk, ky_words, ky_scales, bi, cx_words, cx_scales, wc_words, wc_scales, offs, offs2, out
+):
+    nc = tc.nc
+    with ExitStack() as ctx:
+        keep = ctx.enter_context(tc.tile_pool(name="keep", bufs=1))
+        psum = ctx.enter_context(tc.psum_pool(name="psum", bufs=1))
+
+        tok_list = keep.tile([P, J // 16], U16, name="tok_list")
+        key_list = keep.tile([P, I // 16], U16, name="key_list")
+        x_tiles = [keep.tile([P, n, T], F32, name="x%d" % first) for first, n in XF_LOADS]
+        ky_tab = [keep.tile([P, V], U32, name="ky_tab%d" % a) for a in range(PASSES)]
+        ky_sc_tab = keep.tile([P, PASSES, V], U8, name="ky_sc_tab")
+        cx_codes = keep.tile([P, 2 * J], U8, name="cx_codes", align_bytes=64)
+        wc_codes = keep.tile([P, I], U32, name="wc_codes", align_bytes=64)
+        ctx_sc = keep.tile([P, 2, J], U8, name="ctx_sc", align_bytes=64)
+        factor = keep.tile([P, PASSES, PACK], F32, name="factor")
+        bias_col = keep.tile([P, 2], F32, name="bias_col")
+        ident = keep.tile([P, P], F32, name="ident")
+        picked = keep.tile([P, PLANES, PAD + J], F32, name="picked")
+        step = keep.tile([P, PLANES, J], F32, name="step")
+        u_bf = [keep.tile([P, J, PACK], BF16, name="u_bf%d" % a, align_bytes=64) for a in range(PASSES)]
+        u_codes = [keep.tile([P, J], U32, name="u_codes%d" % a, align_bytes=64) for a in range(PASSES)]
+        u_sc = [keep.tile([P, J], U8, name="u_sc%d" % a, align_bytes=64) for a in range(PASSES)]
+        ky_codes = [keep.tile([P, I], U32, name="ky_codes%d" % a, align_bytes=64) for a in range(PASSES)]
+        ky_sc = keep.tile([P, PASSES, I], U8, name="ky_sc", align_bytes=64)
+        half_q = keep.tile([P, ROW_TILES, I], F32, name="half_q")
+        bias_less_q = keep.tile([P, ROW_TILES, I], F32, name="bias_less_q")
+        gap = keep.tile([P, ROW_TILES, I], F32, name="gap")
+        bent = keep.tile([P, ROW_TILES, I], F32, name="bent")
+        res = keep.tile([P, ROW_TILES, I], F32, name="res")
+
+        bias_ps = psum.tile([P, 2, P], F32, name="bias_ps")
+        q_ps = psum.tile([P, ROW_TILES, I], F32, name="q_ps")
+        a_ps = [psum.tile([P, I], F32, name="a_ps%d" % h) for h in range(ROW_TILES)]
+
+        xv = xf.rearrange("(a p t) n -> a p t n", a=PASSES, t=PACK)
+
+        def load_x(n):
+            first, count = XF_LOADS[n]
+            a, t = divmod(first, PACK)
+            nc.sync.dma_start(x_tiles[n][:], xv[a, :, t : t + count, :])
+
+        nc.vector.memset(ky_sc_tab[:].rearrange("p a v -> p (a v)").bitcast(I32), 0)
+        nc.vector.memset(ctx_sc[:].rearrange("p a v -> p (a v)").bitcast(I32), 0)
+        nc.vector.memset(picked[:, :, PAD - 1 : PAD], 0.0)
+
+        nc.sync.dma_start(key_list[:], offs2)
+        load_x(0)
+        nc.sync.dma_start(tok_list[:], offs)
+        load_x(1)
+        nc.sync.dma_start(wc_codes[:].bitcast(I32), wc_words[0].rearrange("p n t -> p (n t)").bitcast(I32))
+        nc.sync.dma_start(cx_codes[:].bitcast(I32), cx_words[0].bitcast(I32))
+        for n in range(2, len(XF_LOADS)):
+            load_x(n)
+        for a in range(PASSES):
+            nc.sync.dma_start(ky_tab[a][:].bitcast(I32), ky_words[a].rearrange("p n t -> p (n t)").bitcast(I32))
+
+        nc.scalar.dma_start(factor[:], fk.rearrange("(a p t) o -> p a (t o)", a=PASSES, t=PACK))
+        nc.scalar.dma_start(bias_col[:], bi.rearrange("o (p e) -> p (o e)", e=2))
+        for quad in range(4):
+            nc.scalar.dma_start(
+                ky_sc_tab[32 * quad : 32 * quad + 4, :, :].bitcast(I32),
+                ky_scales.bitcast(I32)[:, 4 * quad : 4 * quad + 4, :].rearrange("a r v -> r a v"),
+            )
+        for quad in range(4):
+            nc.scalar.dma_start(
+                ctx_sc[32 * quad : 32 * quad + 4, 1, :].bitcast(I32),
+                wc_scales.bitcast(I32)[0, 4 * quad : 4 * quad + 4, :],
+            )
+        for quad in range(4):
+            nc.gpsimd.dma_start(
+                ctx_sc[32 * quad : 32 * quad + 4, 0, :].bitcast(I32),
+                cx_scales.bitcast(I32)[0, 4 * quad : 4 * quad + 4, :],
+            )
+        make_identity(nc, ident[:])
+
+        for a in range(PASSES):
+            nc.vector.tensor_copy(ky_sc[:, a, :], ky_sc_tab[:, a, :].indirect(key_list[:]))
+
+        def window(plane):
+            for n, (first, count) in enumerate(XF_LOADS):
+                if first <= plane < first + count:
+                    return x_tiles[n][:, plane - first, :]
+
+        def make_plane(plane):
+            a, t = divmod(plane, PACK)
+            if plane < PLANES - 1:
+                nc.scalar.activation(picked[:, plane, PAD:], window(plane).indirect(tok_list[:]), COPY)
+            else:
+                nc.scalar.activation(picked[:, plane, PAD : PAD + P], window(plane).indirect(tok_list[:, 0:8]), COPY)
+                nc.vector.tensor_copy(picked[:, plane, PAD + P :], window(plane).indirect(tok_list[:, 8:16]))
+            nc.vector.scalar_tensor_tensor(
+                step[:, plane, :], picked[:, plane, PAD - 1 : PAD - 1 + J], -0.6, picked[:, plane, PAD:],
+                ALU.mult, ALU.add,
+            )
+            nc.vector.tensor_scalar(u_bf[a][:, :, t], step[:, plane, :], factor[:, a, t : t + 1], None, ALU.mult)
+
+        def quantize(a):
+            nc.vector.quantize_mx(
+                out=u_codes[a][:].bitcast(E5M2X4), scales=u_sc[a][:], in_=u_bf[a][:].rearrange("p j t -> p (j t)")
+            )
+
+        def gather_keys(a):
+            nc.vector.tensor_copy(ky_codes[a][:], ky_tab[a][:].indirect(key_list[:]))
+
+        def score_pass(a):
+            for h in range(ROW_TILES):
+                rows = slice(h * P, (h + 1) * P)
+                nc.tensor.matmul_mx(
+                    out=a_ps[h][:],
+                    lhsT=u_codes[a][:, rows].bitcast(E5M2X4), lhsT_scale=u_sc[a][:, rows],
+                    rhs=ky_codes[a][:].bitcast(E5M2X4), rhs_scale=ky_sc[:, a, :],
+                    start=(a == 0), stop=(a == PASSES - 1),
+                )
+
+        for plane in range(PACK):
+            make_plane(plane)
+
+        for e in range(2):
+            nc.tensor.transpose(bias_ps[:, e, :], bias_col[:, e : e + 1].to_broadcast([P, P]), ident[:])
+        for h in range(ROW_TILES):
+            nc.tensor.matmul_mx(
+                out=q_ps[:, h, :],
+                lhsT=cx_codes[:, 2 * h * P : 2 * (h + 1) * P].bitcast(E2M1X4),
+                lhsT_scale=ctx_sc[:, 0, h * P : (h + 1) * P],
+                rhs=wc_codes[:].bitcast(E4M3X4), rhs_scale=ctx_sc[:, 1, :],
+                start=True, stop=True,
+            )
+        nc.scalar.activation(half_q[:], q_ps[:], COPY, scale=0.5)
+
+        make_plane(PACK)
+        quantize(0)
+        for h in range(ROW_TILES):
+            nc.vector.scalar_tensor_tensor(
+                bias_less_q[:, h, :].rearrange("m (p e) -> m p e", e=2),
+                half_q[:, h, :].rearrange("m (p e) -> m p e", e=2),
+                -2.0,
+                bias_ps[:].rearrange("m e p -> m p e"),
+                ALU.mult, ALU.add,
+            )
+        for plane in range(PACK + 1, PLANES):
+            make_plane(plane)
+        gather_keys(0)
+        score_pass(0)
+        quantize(1)
+        gather_keys(1)
+        score_pass(1)
+
+        for h in range(ROW_TILES):
+            nc.vector.tensor_tensor(gap[:, h, :], a_ps[h][:], bias_less_q[:, h, :], ALU.add)
+        for h in range(ROW_TILES):
+            nc.vector.scalar_tensor_tensor(bent[:, h, :], gap[:, h, :], -0.5, gap[:, h, :], ALU.mult, ALU.max)
+        for h in range(ROW_TILES):
+            nc.vector.tensor_tensor(res[:, h, :], bent[:, h, :], half_q[:, h, :], ALU.add)
+            nc.sync.dma_start(out[h * P : (h + 1) * P, :], res[:, h, :])

@@ -24,7 +24,7 @@ PASSES = K // (P * PACK)
 PLANES = PASSES * PACK
 PAD = 8
 ROW_TILES = J // P
-XF_LOADS = [(0, 2), (2, 2), (4, 1), (5, 1), (6, 1), (7, 1)]
+SMALL_BEFORE = [0, 2, 3, 2, 3, 2, 3, 1]
 
 
 def tile_list_scores_steps_listed_tworank_kernel(
@@ -37,8 +37,8 @@ def tile_list_scores_steps_listed_tworank_kernel(
 
         tok_list = keep.tile([P, J // 16], U16, name="tok_list")
         key_list = keep.tile([P, I // 16], U16, name="key_list")
-        x_tiles = [keep.tile([P, n, T], F32, name="x%d" % first) for first, n in XF_LOADS]
-        ky_tab = [keep.tile([P, V], U32, name="ky_tab%d" % a) for a in range(PASSES)]
+        x_tiles = [keep.tile([P, T], F32, name="x%d" % plane, tag="x%d" % plane) for plane in range(PLANES)]
+        ky_tab = [keep.tile([P, V], U32, name="ky_tab%d" % a, tag="ky_tab%d" % a) for a in range(PASSES)]
         ky_sc_tab = keep.tile([P, PASSES, V], U8, name="ky_sc_tab")
         cx_codes = keep.tile([P, 2 * J], U8, name="cx_codes", align_bytes=64)
         wc_codes = keep.tile([P, I], U32, name="wc_codes", align_bytes=64)
@@ -46,15 +46,13 @@ def tile_list_scores_steps_listed_tworank_kernel(
         factor = keep.tile([P, PASSES, PACK], F32, name="factor")
         bias_col = keep.tile([P, 2], F32, name="bias_col")
         ident = keep.tile([P, P], F32, name="ident")
-        picked = keep.tile([P, PLANES, PAD + J], F32, name="picked")
-        step = keep.tile([P, PLANES, J], F32, name="step")
+        work = keep.tile([P, PLANES, J], F32, name="work")
+        lined = keep.tile([P, PLANES, PAD + J], F32, name="lined")
         u_bf = [keep.tile([P, J, PACK], BF16, name="u_bf%d" % a, align_bytes=64) for a in range(PASSES)]
         u_codes = [keep.tile([P, J], U32, name="u_codes%d" % a, align_bytes=64) for a in range(PASSES)]
         u_sc = [keep.tile([P, J], U8, name="u_sc%d" % a, align_bytes=64) for a in range(PASSES)]
         ky_codes = [keep.tile([P, I], U32, name="ky_codes%d" % a, align_bytes=64) for a in range(PASSES)]
         ky_sc = keep.tile([P, PASSES, I], U8, name="ky_sc", align_bytes=64)
-        half_q = keep.tile([P, ROW_TILES, I], F32, name="half_q")
-        bias_less_q = keep.tile([P, ROW_TILES, I], F32, name="bias_less_q")
         gap = keep.tile([P, ROW_TILES, I], F32, name="gap")
         bent = keep.tile([P, ROW_TILES, I], F32, name="bent")
         res = keep.tile([P, ROW_TILES, I], F32, name="res")
@@ -65,65 +63,73 @@ def tile_list_scores_steps_listed_tworank_kernel(
 
         xv = xf.rearrange("(a p t) n -> a p t n", a=PASSES, t=PACK)
 
-        def load_x(n):
-            first, count = XF_LOADS[n]
-            a, t = divmod(first, PACK)
-            nc.sync.dma_start(x_tiles[n][:], xv[a, :, t : t + count, :])
-
+        zeros = keep.tile([P, PLANES], F32, name="zeros")
+        nc.vector.memset(zeros[:], 0.0)
         nc.vector.memset(ky_sc_tab[:].rearrange("p a v -> p (a v)").bitcast(I32), 0)
-        nc.vector.memset(ctx_sc[:].rearrange("p a v -> p (a v)").bitcast(I32), 0)
-        nc.vector.memset(picked[:, :, PAD - 1 : PAD], 0.0)
+        nc.gpsimd.memset(ctx_sc[:].rearrange("p a v -> p (a v)").bitcast(I32), 0)
+        make_identity(nc, ident[:])
+        nc.scalar.activation(lined[:, :, PAD - 1], zeros[:], COPY)
 
-        nc.sync.dma_start(key_list[:], offs2)
-        load_x(0)
-        nc.sync.dma_start(tok_list[:], offs)
-        load_x(1)
-        nc.sync.dma_start(wc_codes[:].bitcast(I32), wc_words[0].rearrange("p n t -> p (n t)").bitcast(I32))
-        nc.sync.dma_start(cx_codes[:].bitcast(I32), cx_words[0].bitcast(I32))
-        for n in range(2, len(XF_LOADS)):
-            load_x(n)
+
+        small = [
+            (tok_list[:], offs),
+            (factor[:], fk.rearrange("(a p t) o -> p a (t o)", a=PASSES, t=PACK)),
+            (key_list[:], offs2),
+        ]
+        for quad in range(4):
+            small.append((
+                ky_sc_tab[32 * quad : 32 * quad + 4, :, :].bitcast(I32),
+                ky_scales.bitcast(I32)[:, 4 * quad : 4 * quad + 4, :].rearrange("a r v -> r a v"),
+            ))
+        small.append((bias_col[:], bi.rearrange("o (p e) -> p (o e)", e=2)))
+        for side, scales in enumerate((cx_scales, wc_scales)):
+            for quad in range(4):
+                small.append((
+                    ctx_sc[32 * quad : 32 * quad + 4, side, :].bitcast(I32),
+                    scales.bitcast(I32)[0, 4 * quad : 4 * quad + 4, :],
+                ))
+        small.append((wc_codes[:].bitcast(I32), wc_words[0].rearrange("p n t -> p (n t)").bitcast(I32)))
+        small.append((cx_codes[:].bitcast(I32), cx_words[0].bitcast(I32)))
+        done = 0
+        for plane in range(PLANES):
+            for dst, src in small[done : done + SMALL_BEFORE[plane]]:
+                nc.sync.dma_start(dst, src)
+            done = done + SMALL_BEFORE[plane]
+            a, t = divmod(plane, PACK)
+            nc.sync.dma_start(x_tiles[plane][:], xv[a, :, t, :])
+        for dst, src in small[done:]:
+            nc.sync.dma_start(dst, src)
         for a in range(PASSES):
             nc.sync.dma_start(ky_tab[a][:].bitcast(I32), ky_words[a].rearrange("p n t -> p (n t)").bitcast(I32))
 
-        nc.scalar.dma_start(factor[:], fk.rearrange("(a p t) o -> p a (t o)", a=PASSES, t=PACK))
-        nc.scalar.dma_start(bias_col[:], bi.rearrange("o (p e) -> p (o e)", e=2))
-        for quad in range(4):
-            nc.scalar.dma_start(
-                ky_sc_tab[32 * quad : 32 * quad + 4, :, :].bitcast(I32),
-                ky_scales.bitcast(I32)[:, 4 * quad : 4 * quad + 4, :].rearrange("a r v -> r a v"),
-            )
-        for quad in range(4):
-            nc.scalar.dma_start(
-                ctx_sc[32 * quad : 32 * quad + 4, 1, :].bitcast(I32),
-                wc_scales.bitcast(I32)[0, 4 * quad : 4 * quad + 4, :],
-            )
-        for quad in range(4):
-            nc.gpsimd.dma_start(
-                ctx_sc[32 * quad : 32 * quad + 4, 0, :].bitcast(I32),
-                cx_scales.bitcast(I32)[0, 4 * quad : 4 * quad + 4, :],
-            )
-        make_identity(nc, ident[:])
-
-        for a in range(PASSES):
-            nc.vector.tensor_copy(ky_sc[:, a, :], ky_sc_tab[:, a, :].indirect(key_list[:]))
-
         def window(plane):
-            for n, (first, count) in enumerate(XF_LOADS):
-                if first <= plane < first + count:
-                    return x_tiles[n][:, plane - first, :]
+            return x_tiles[plane][:]
+
+        def make_pair(pair):
+            a, t = divmod(2 * pair, PACK)
+            even = 2 * pair
+            for e in range(2):
+                if even + e in (0, 2):
+                    nc.vector.tensor_copy(work[:, even + e, :], window(even + e).indirect(tok_list[:]))
+                else:
+                    nc.scalar.activation(work[:, even + e, :], window(even + e).indirect(tok_list[:]), COPY)
+                nc.scalar.activation(
+                    lined[:, even + e, PAD:], work[:, even + e, :], COPY, scale=factor[:, a, t + e : t + e + 1]
+                )
+            both = lined[:, even : even + 2, :].rearrange("p e j -> p j e")
+            nc.vector.scalar_tensor_tensor(
+                u_bf[a][:, :, t : t + 2], both[:, PAD - 1 : PAD - 1 + J, :], -0.6, both[:, PAD:, :],
+                ALU.mult, ALU.add,
+            )
 
         def make_plane(plane):
             a, t = divmod(plane, PACK)
-            if plane < PLANES - 1:
-                nc.scalar.activation(picked[:, plane, PAD:], window(plane).indirect(tok_list[:]), COPY)
-            else:
-                nc.scalar.activation(picked[:, plane, PAD : PAD + P], window(plane).indirect(tok_list[:, 0:8]), COPY)
-                nc.vector.tensor_copy(picked[:, plane, PAD + P :], window(plane).indirect(tok_list[:, 8:16]))
+            nc.scalar.activation(lined[:, plane, PAD:], window(plane).indirect(tok_list[:]), COPY)
             nc.vector.scalar_tensor_tensor(
-                step[:, plane, :], picked[:, plane, PAD - 1 : PAD - 1 + J], -0.6, picked[:, plane, PAD:],
+                work[:, plane, :], lined[:, plane, PAD - 1 : PAD - 1 + J], -0.6, lined[:, plane, PAD:],
                 ALU.mult, ALU.add,
             )
-            nc.vector.tensor_scalar(u_bf[a][:, :, t], step[:, plane, :], factor[:, a, t : t + 1], None, ALU.mult)
+            nc.vector.tensor_scalar(u_bf[a][:, :, t], work[:, plane, :], factor[:, a, t : t + 1], None, ALU.mult)
 
         def quantize(a):
             nc.vector.quantize_mx(
@@ -143,7 +149,12 @@ def tile_list_scores_steps_listed_tworank_kernel(
                     start=(a == 0), stop=(a == PASSES - 1),
                 )
 
-        for plane in range(PACK):
+        make_pair(0)
+        for a in range(PASSES):
+            nc.vector.tensor_copy(ky_sc[:, a, :], ky_sc_tab[:, a, :].indirect(key_list[:]))
+        make_pair(1)
+        quantize(0)
+        for plane in range(PACK, PLANES):
             make_plane(plane)
 
         for e in range(2):
@@ -156,10 +167,16 @@ def tile_list_scores_steps_listed_tworank_kernel(
                 rhs=wc_codes[:].bitcast(E4M3X4), rhs_scale=ctx_sc[:, 1, :],
                 start=True, stop=True,
             )
+        half_q = keep.tile([P, ROW_TILES, I], F32, name="half_q", tag="x%d" % (PLANES - 1))
         nc.scalar.activation(half_q[:], q_ps[:], COPY, scale=0.5)
 
-        make_plane(PACK)
-        quantize(0)
+        gather_keys(0)
+        score_pass(0)
+        quantize(1)
+        gather_keys(1)
+        score_pass(1)
+
+        bias_less_q = keep.tile([P, ROW_TILES, I], F32, name="bias_less_q", tag="ky_tab%d" % (PASSES - 1))
         for h in range(ROW_TILES):
             nc.vector.scalar_tensor_tensor(
                 bias_less_q[:, h, :].rearrange("m (p e) -> m p e", e=2),
@@ -168,14 +185,6 @@ def tile_list_scores_steps_listed_tworank_kernel(
                 bias_ps[:].rearrange("m e p -> m p e"),
                 ALU.mult, ALU.add,
             )
-        for plane in range(PACK + 1, PLANES):
-            make_plane(plane)
-        gather_keys(0)
-        score_pass(0)
-        quantize(1)
-        gather_keys(1)
-        score_pass(1)
-
         for h in range(ROW_TILES):
             nc.vector.tensor_tensor(gap[:, h, :], a_ps[h][:], bias_less_q[:, h, :], ALU.add)
         for h in range(ROW_TILES):

@@ -37,7 +37,7 @@ def tile_list_scores_steps_listed_tworank_kernel(
 
         tok_list = keep.tile([P, J // 16], U16, name="tok_list")
         key_list = keep.tile([P, I // 16], U16, name="key_list")
-        x_tiles = [keep.tile([P, T], F32, name="x%d" % plane, tag="x%d" % plane) for plane in range(PLANES)]
+        x_tiles = [keep.tile([P, T], F32, name="x%d" % plane) for plane in range(PLANES)]
         ky_tab = [keep.tile([P, V], U32, name="ky_tab%d" % a, tag="ky_tab%d" % a) for a in range(PASSES)]
         ky_sc_tab = keep.tile([P, PASSES, V], U8, name="ky_sc_tab")
         cx_codes = keep.tile([P, 2 * J], U8, name="cx_codes", align_bytes=64)
@@ -45,9 +45,11 @@ def tile_list_scores_steps_listed_tworank_kernel(
         ctx_sc = keep.tile([P, 2, J], U8, name="ctx_sc", align_bytes=64)
         factor = keep.tile([P, PASSES, PACK], F32, name="factor")
         bias_col = keep.tile([P, 2], F32, name="bias_col")
+        bias_row = keep.tile([P, I], F32, name="bias_row")
         ident = keep.tile([P, P], F32, name="ident")
         work = keep.tile([P, PLANES, J], F32, name="work")
         lined = keep.tile([P, PLANES, PAD + J], F32, name="lined")
+        flat = keep.tile([P, PLANES, J], BF16, name="flat")
         u_bf = [keep.tile([P, J, PACK], BF16, name="u_bf%d" % a, align_bytes=64) for a in range(PASSES)]
         u_codes = [keep.tile([P, J], U32, name="u_codes%d" % a, align_bytes=64) for a in range(PASSES)]
         u_sc = [keep.tile([P, J], U8, name="u_sc%d" % a, align_bytes=64) for a in range(PASSES)]
@@ -97,43 +99,56 @@ def tile_list_scores_steps_listed_tworank_kernel(
             done = done + SMALL_BEFORE[plane]
             a, t = divmod(plane, PACK)
             nc.sync.dma_start(x_tiles[plane][:], xv[a, :, t, :])
+        nc.sync.dma_start(ky_tab[0][:].bitcast(I32), ky_words[0].rearrange("p n t -> p (n t)").bitcast(I32))
         for dst, src in small[done:]:
             nc.sync.dma_start(dst, src)
-        for a in range(PASSES):
-            nc.sync.dma_start(ky_tab[a][:].bitcast(I32), ky_words[a].rearrange("p n t -> p (n t)").bitcast(I32))
+        nc.sync.dma_start(ky_tab[1][:].bitcast(I32), ky_words[1].rearrange("p n t -> p (n t)").bitcast(I32))
 
-        def window(plane):
-            return x_tiles[plane][:]
-
-        def make_pair(pair):
-            a, t = divmod(2 * pair, PACK)
-            even = 2 * pair
-            for e in range(2):
-                if even + e in (0, 2):
-                    nc.vector.tensor_copy(work[:, even + e, :], window(even + e).indirect(tok_list[:]))
-                else:
-                    nc.scalar.activation(work[:, even + e, :], window(even + e).indirect(tok_list[:]), COPY)
-                nc.scalar.activation(
-                    lined[:, even + e, PAD:], work[:, even + e, :], COPY, scale=factor[:, a, t + e : t + e + 1]
-                )
-            both = lined[:, even : even + 2, :].rearrange("p e j -> p j e")
+        def take_step(dst, plane, first, count):
             nc.vector.scalar_tensor_tensor(
-                u_bf[a][:, :, t : t + 2], both[:, PAD - 1 : PAD - 1 + J, :], -0.6, both[:, PAD:, :],
-                ALU.mult, ALU.add,
+                dst[:, plane, first : first + count],
+                lined[:, plane, PAD - 1 + first : PAD - 1 + first + count], -0.6,
+                lined[:, plane, PAD + first : PAD + first + count], ALU.mult, ALU.add,
             )
 
-        def make_plane(plane):
+        def factor_first(plane, parts):
             a, t = divmod(plane, PACK)
-            nc.scalar.activation(lined[:, plane, PAD:], window(plane).indirect(tok_list[:]), COPY)
-            nc.vector.scalar_tensor_tensor(
-                work[:, plane, :], lined[:, plane, PAD - 1 : PAD - 1 + J], -0.6, lined[:, plane, PAD:],
-                ALU.mult, ALU.add,
-            )
-            nc.vector.tensor_scalar(u_bf[a][:, :, t], work[:, plane, :], factor[:, a, t : t + 1], None, ALU.mult)
+            count = J // parts
+            for first in range(0, J, count):
+                nc.scalar.activation(
+                    work[:, plane, first : first + count],
+                    x_tiles[plane][:].indirect(tok_list[:, first // 16 : (first + count) // 16]), COPY,
+                )
+            for first in range(0, J, count):
+                nc.scalar.activation(
+                    lined[:, plane, PAD + first : PAD + first + count], work[:, plane, first : first + count],
+                    COPY, scale=factor[:, a, t : t + 1],
+                )
+            for first in range(0, J, count):
+                take_step(flat, plane, first, count)
 
-        def quantize(a):
+        def step_first(plane):
+            a, t = divmod(plane, PACK)
+            nc.scalar.activation(lined[:, plane, PAD:], x_tiles[plane][:].indirect(tok_list[:]), COPY)
+            take_step(work, plane, 0, J)
+            nc.vector.tensor_scalar(flat[:, plane, :], work[:, plane, :], factor[:, a, t : t + 1], None, ALU.mult)
+
+        def make_flat(plane):
+            if plane in (0, 2, 4):
+                factor_first(plane, 1)
+            else:
+                step_first(plane)
+
+        def weave(a, first, count):
+            nc.vector.tensor_copy(
+                u_bf[a][:, first : first + count, :].rearrange("p (c i) t -> p c t i", i=4),
+                flat[:, a * PACK : (a + 1) * PACK, first : first + count].rearrange("p t (c i) -> p c t i", i=4),
+            )
+
+        def quantize(a, first, count):
             nc.vector.quantize_mx(
-                out=u_codes[a][:].bitcast(E5M2X4), scales=u_sc[a][:], in_=u_bf[a][:].rearrange("p j t -> p (j t)")
+                out=u_codes[a][:, first : first + count].bitcast(E5M2X4), scales=u_sc[a][:, first : first + count],
+                in_=u_bf[a][:, first : first + count, :].rearrange("p j t -> p (j t)"),
             )
 
         def gather_keys(a):
@@ -149,16 +164,26 @@ def tile_list_scores_steps_listed_tworank_kernel(
                     start=(a == 0), stop=(a == PASSES - 1),
                 )
 
-        make_pair(0)
+        for plane in range(PACK):
+            make_flat(plane)
         for a in range(PASSES):
             nc.vector.tensor_copy(ky_sc[:, a, :], ky_sc_tab[:, a, :].indirect(key_list[:]))
-        make_pair(1)
-        quantize(0)
-        for plane in range(PACK, PLANES):
-            make_plane(plane)
+        weave(0, 0, J)
+        make_flat(PACK)
+        quantize(0, 0, J)
+        for plane in range(PACK + 1, PLANES - 1):
+            make_flat(plane)
+        factor_first(PLANES - 1, ROW_TILES)
+        gather_keys(0)
+        score_pass(0)
+        for h in range(ROW_TILES):
+            weave(1, h * P, P)
+        for h in range(ROW_TILES):
+            quantize(1, h * P, P)
 
         for e in range(2):
             nc.tensor.transpose(bias_ps[:, e, :], bias_col[:, e : e + 1].to_broadcast([P, P]), ident[:])
+        nc.scalar.copy(bias_row[:].rearrange("m (p e) -> m p e", e=2), bias_ps[:].rearrange("m e p -> m p e"))
         for h in range(ROW_TILES):
             nc.tensor.matmul_mx(
                 out=q_ps[:, h, :],
@@ -167,24 +192,15 @@ def tile_list_scores_steps_listed_tworank_kernel(
                 rhs=wc_codes[:].bitcast(E4M3X4), rhs_scale=ctx_sc[:, 1, :],
                 start=True, stop=True,
             )
-        half_q = keep.tile([P, ROW_TILES, I], F32, name="half_q", tag="x%d" % (PLANES - 1))
+        half_q = keep.tile([P, ROW_TILES, I], F32, name="half_q")
         nc.scalar.activation(half_q[:], q_ps[:], COPY, scale=0.5)
 
-        gather_keys(0)
-        score_pass(0)
-        quantize(1)
         gather_keys(1)
         score_pass(1)
 
         bias_less_q = keep.tile([P, ROW_TILES, I], F32, name="bias_less_q", tag="ky_tab%d" % (PASSES - 1))
         for h in range(ROW_TILES):
-            nc.vector.scalar_tensor_tensor(
-                bias_less_q[:, h, :].rearrange("m (p e) -> m p e", e=2),
-                half_q[:, h, :].rearrange("m (p e) -> m p e", e=2),
-                -2.0,
-                bias_ps[:].rearrange("m e p -> m p e"),
-                ALU.mult, ALU.add,
-            )
+            nc.vector.tensor_tensor(bias_less_q[:, h, :], bias_row[:], q_ps[:, h, :], ALU.subtract)
         for h in range(ROW_TILES):
             nc.vector.tensor_tensor(gap[:, h, :], a_ps[h][:], bias_less_q[:, h, :], ALU.add)
         for h in range(ROW_TILES):

@@ -24,7 +24,7 @@ PASSES = K // (P * PACK)
 PLANES = PASSES * PACK
 PAD = 8
 ROW_TILES = J // P
-SMALL_BEFORE = [0, 2, 3, 2, 3, 2, 3, 1]
+PAIRS = 3
 
 
 def tile_list_scores_steps_listed_tworank_kernel(
@@ -37,12 +37,14 @@ def tile_list_scores_steps_listed_tworank_kernel(
 
         tok_list = keep.tile([P, J // 16], U16, name="tok_list")
         key_list = keep.tile([P, I // 16], U16, name="key_list")
-        x_tiles = [keep.tile([P, T], F32, name="x%d" % plane) for plane in range(PLANES)]
+        x_pairs = [keep.tile([P, 2, T], F32, name="x_pair%d" % n) for n in range(PAIRS)]
+        x_last = [keep.tile([P, T], F32, name="x_last%d" % n) for n in range(2)]
+        x_rows = [x_pairs[n][:, e, :] for n in range(PAIRS) for e in range(2)] + [x_last[0][:], x_last[1][:]]
         ky_tab = [keep.tile([P, V], U32, name="ky_tab%d" % a, tag="ky_tab%d" % a) for a in range(PASSES)]
         ky_sc_tab = keep.tile([P, PASSES, V], U8, name="ky_sc_tab")
         cx_codes = keep.tile([P, 2 * J], U8, name="cx_codes", align_bytes=64)
         wc_codes = keep.tile([P, I], U32, name="wc_codes", align_bytes=64)
-        ctx_sc = keep.tile([P, 2, J], U8, name="ctx_sc", align_bytes=64)
+        scales = keep.tile([P, 4, J], U8, name="scales", align_bytes=64)
         factor = keep.tile([P, PASSES, PACK], F32, name="factor")
         bias_col = keep.tile([P, 2], F32, name="bias_col")
         bias_row = keep.tile([P, I], F32, name="bias_row")
@@ -54,7 +56,8 @@ def tile_list_scores_steps_listed_tworank_kernel(
         u_codes = [keep.tile([P, J], U32, name="u_codes%d" % a, align_bytes=64) for a in range(PASSES)]
         u_sc = [keep.tile([P, J], U8, name="u_sc%d" % a, align_bytes=64) for a in range(PASSES)]
         ky_codes = [keep.tile([P, I], U32, name="ky_codes%d" % a, align_bytes=64) for a in range(PASSES)]
-        ky_sc = keep.tile([P, PASSES, I], U8, name="ky_sc", align_bytes=64)
+        ky_sc = keep.tile([P, PASSES, I], U8, name="ky_sc")
+        half_q = keep.tile([P, ROW_TILES, I], F32, name="half_q")
         gap = keep.tile([P, ROW_TILES, I], F32, name="gap")
         bent = keep.tile([P, ROW_TILES, I], F32, name="bent")
         res = keep.tile([P, ROW_TILES, I], F32, name="res")
@@ -66,43 +69,44 @@ def tile_list_scores_steps_listed_tworank_kernel(
         xv = xf.rearrange("(a p t) n -> a p t n", a=PASSES, t=PACK)
 
         zeros = keep.tile([P, PLANES], F32, name="zeros")
-        nc.vector.memset(zeros[:], 0.0)
-        nc.vector.memset(ky_sc_tab[:].rearrange("p a v -> p (a v)").bitcast(I32), 0)
-        nc.gpsimd.memset(ctx_sc[:].rearrange("p a v -> p (a v)").bitcast(I32), 0)
+        nc.gpsimd.memset(ky_sc_tab[:].rearrange("p a v -> p (a v)").bitcast(I32), 0)
+        nc.gpsimd.memset(scales[:, 2:4, :].rearrange("p a v -> p (a v)").bitcast(I32), 0)
+        nc.gpsimd.memset(zeros[:], 0.0)
         make_identity(nc, ident[:])
+
+        nc.scalar.dma_start(ky_sc_tab[0:P:8, :, :].bitcast(I32), ky_scales.bitcast(I32).rearrange("a q v -> q a v"))
+        nc.scalar.dma_start(scales[0:P:8, 2, :].bitcast(I32), cx_scales.bitcast(I32)[0])
+        nc.scalar.dma_start(scales[0:P:8, 3, :].bitcast(I32), wc_scales.bitcast(I32)[0])
         nc.scalar.activation(lined[:, :, PAD - 1], zeros[:], COPY)
 
+        def load_pair(n):
+            a, t = divmod(2 * n, PACK)
+            nc.sync.dma_start(x_pairs[n][:], xv[a, :, t : t + 2, :])
 
-        small = [
-            (tok_list[:], offs),
-            (factor[:], fk.rearrange("(a p t) o -> p a (t o)", a=PASSES, t=PACK)),
-            (key_list[:], offs2),
-        ]
-        for quad in range(4):
-            small.append((
-                ky_sc_tab[32 * quad : 32 * quad + 4, :, :].bitcast(I32),
-                ky_scales.bitcast(I32)[:, 4 * quad : 4 * quad + 4, :].rearrange("a r v -> r a v"),
-            ))
-        small.append((bias_col[:], bi.rearrange("o (p e) -> p (o e)", e=2)))
-        for side, scales in enumerate((cx_scales, wc_scales)):
-            for quad in range(4):
-                small.append((
-                    ctx_sc[32 * quad : 32 * quad + 4, side, :].bitcast(I32),
-                    scales.bitcast(I32)[0, 4 * quad : 4 * quad + 4, :],
-                ))
-        small.append((wc_codes[:].bitcast(I32), wc_words[0].rearrange("p n t -> p (n t)").bitcast(I32)))
-        small.append((cx_codes[:].bitcast(I32), cx_words[0].bitcast(I32)))
-        done = 0
-        for plane in range(PLANES):
-            for dst, src in small[done : done + SMALL_BEFORE[plane]]:
-                nc.sync.dma_start(dst, src)
-            done = done + SMALL_BEFORE[plane]
-            a, t = divmod(plane, PACK)
-            nc.sync.dma_start(x_tiles[plane][:], xv[a, :, t, :])
-        nc.sync.dma_start(ky_tab[0][:].bitcast(I32), ky_words[0].rearrange("p n t -> p (n t)").bitcast(I32))
-        for dst, src in small[done:]:
-            nc.sync.dma_start(dst, src)
-        nc.sync.dma_start(ky_tab[1][:].bitcast(I32), ky_words[1].rearrange("p n t -> p (n t)").bitcast(I32))
+        nc.sync.dma_start(key_list[:], offs2)
+        load_pair(0)
+        nc.sync.dma_start(tok_list[:], offs)
+        nc.sync.dma_start(factor[:], fk.rearrange("(a p t) o -> p a (t o)", a=PASSES, t=PACK))
+        nc.sync.dma_start(bias_col[:], bi.rearrange("o (p e) -> p (o e)", e=2))
+        load_pair(1)
+        load_pair(2)
+        nc.sync.dma_start(x_last[0][:], xv[PASSES - 1, :, 2, :])
+
+        for a in range(PASSES):
+            nc.vector.tensor_copy(ky_sc[:, a, :], ky_sc_tab[:, a, :].indirect(key_list[:]))
+        nc.vector.tensor_copy(
+            scales[:, 0:2, :].rearrange("p a v -> p (a v)").bitcast(I32),
+            ky_sc[:].rearrange("p a v -> p (a v)").bitcast(I32),
+        )
+        scale_words = scales[:].rearrange("p a v -> p (a v)").bitcast(I32)
+        for r in range(1, 4):
+            nc.sync.dma_start(scale_words[r:P:32, :], scale_words[8 * r : P : 32, :])
+
+        nc.sync.dma_start(x_last[1][:], xv[PASSES - 1, :, 3, :])
+        nc.sync.dma_start(wc_codes[:].bitcast(I32), wc_words[0].rearrange("p n t -> p (n t)").bitcast(I32))
+        nc.sync.dma_start(cx_codes[:].bitcast(I32), cx_words[0].bitcast(I32))
+        for a in range(PASSES):
+            nc.sync.dma_start(ky_tab[a][:].bitcast(I32), ky_words[a].rearrange("p n t -> p (n t)").bitcast(I32))
 
         def take_step(dst, plane, first, count):
             nc.vector.scalar_tensor_tensor(
@@ -111,33 +115,23 @@ def tile_list_scores_steps_listed_tworank_kernel(
                 lined[:, plane, PAD + first : PAD + first + count], ALU.mult, ALU.add,
             )
 
-        def factor_first(plane, parts):
-            a, t = divmod(plane, PACK)
-            count = J // parts
-            for first in range(0, J, count):
-                nc.scalar.activation(
-                    work[:, plane, first : first + count],
-                    x_tiles[plane][:].indirect(tok_list[:, first // 16 : (first + count) // 16]), COPY,
-                )
-            for first in range(0, J, count):
-                nc.scalar.activation(
-                    lined[:, plane, PAD + first : PAD + first + count], work[:, plane, first : first + count],
-                    COPY, scale=factor[:, a, t : t + 1],
-                )
-            for first in range(0, J, count):
-                take_step(flat, plane, first, count)
+        def gather_tokens(dst, plane, first, count):
+            nc.scalar.activation(dst, x_rows[plane].indirect(tok_list[:, first // 16 : (first + count) // 16]), COPY)
 
-        def step_first(plane):
+        def factor_of(plane):
             a, t = divmod(plane, PACK)
-            nc.scalar.activation(lined[:, plane, PAD:], x_tiles[plane][:].indirect(tok_list[:]), COPY)
+            return factor[:, a, t : t + 1]
+
+        def factor_then_step(plane, first, count):
+            nc.scalar.activation(
+                lined[:, plane, PAD + first : PAD + first + count], work[:, plane, first : first + count],
+                COPY, scale=factor_of(plane),
+            )
+            take_step(flat, plane, first, count)
+
+        def step_then_factor(plane):
             take_step(work, plane, 0, J)
-            nc.vector.tensor_scalar(flat[:, plane, :], work[:, plane, :], factor[:, a, t : t + 1], None, ALU.mult)
-
-        def make_flat(plane):
-            if plane in (0, 2, 4):
-                factor_first(plane, 1)
-            else:
-                step_first(plane)
+            nc.vector.tensor_scalar(flat[:, plane, :], work[:, plane, :], factor_of(plane), None, ALU.mult)
 
         def weave(a, first, count):
             nc.vector.tensor_copy(
@@ -160,47 +154,54 @@ def tile_list_scores_steps_listed_tworank_kernel(
                 nc.tensor.matmul_mx(
                     out=a_ps[h][:],
                     lhsT=u_codes[a][:, rows].bitcast(E5M2X4), lhsT_scale=u_sc[a][:, rows],
-                    rhs=ky_codes[a][:].bitcast(E5M2X4), rhs_scale=ky_sc[:, a, :],
+                    rhs=ky_codes[a][:].bitcast(E5M2X4), rhs_scale=scales[:, a, :],
                     start=(a == 0), stop=(a == PASSES - 1),
                 )
 
-        for plane in range(PACK):
-            make_flat(plane)
-        for a in range(PASSES):
-            nc.vector.tensor_copy(ky_sc[:, a, :], ky_sc_tab[:, a, :].indirect(key_list[:]))
+        for e in range(2):
+            nc.tensor.transpose(bias_ps[:, e, :], bias_col[:, e : e + 1].to_broadcast([P, P]), ident[:])
+        nc.scalar.copy(bias_row[:].rearrange("m (p e) -> m p e", e=2), bias_ps[:].rearrange("m e p -> m p e"))
+
+        for even in (0, 2):
+            gather_tokens(work[:, even, :], even, 0, J)
+            gather_tokens(lined[:, even + 1, PAD:], even + 1, 0, J)
+            factor_then_step(even, 0, J)
+            step_then_factor(even + 1)
         weave(0, 0, J)
-        make_flat(PACK)
+
         quantize(0, 0, J)
-        for plane in range(PACK + 1, PLANES - 1):
-            make_flat(plane)
-        factor_first(PLANES - 1, ROW_TILES)
-        gather_keys(0)
-        score_pass(0)
+
+        for plane in range(PACK, PLANES - 1):
+            gather_tokens(lined[:, plane, PAD:], plane, 0, J)
+        for plane in range(PACK, PLANES - 1):
+            step_then_factor(plane)
+        for h in range(ROW_TILES):
+            gather_tokens(work[:, PLANES - 1, h * P : (h + 1) * P], PLANES - 1, h * P, P)
+        for h in range(ROW_TILES):
+            factor_then_step(PLANES - 1, h * P, P)
         for h in range(ROW_TILES):
             weave(1, h * P, P)
         for h in range(ROW_TILES):
             quantize(1, h * P, P)
 
-        for e in range(2):
-            nc.tensor.transpose(bias_ps[:, e, :], bias_col[:, e : e + 1].to_broadcast([P, P]), ident[:])
-        nc.scalar.copy(bias_row[:].rearrange("m (p e) -> m p e", e=2), bias_ps[:].rearrange("m e p -> m p e"))
         for h in range(ROW_TILES):
             nc.tensor.matmul_mx(
                 out=q_ps[:, h, :],
                 lhsT=cx_codes[:, 2 * h * P : 2 * (h + 1) * P].bitcast(E2M1X4),
-                lhsT_scale=ctx_sc[:, 0, h * P : (h + 1) * P],
-                rhs=wc_codes[:].bitcast(E4M3X4), rhs_scale=ctx_sc[:, 1, :],
+                lhsT_scale=scales[:, 2, h * P : (h + 1) * P],
+                rhs=wc_codes[:].bitcast(E4M3X4), rhs_scale=scales[:, 3, :],
                 start=True, stop=True,
             )
-        half_q = keep.tile([P, ROW_TILES, I], F32, name="half_q")
         nc.scalar.activation(half_q[:], q_ps[:], COPY, scale=0.5)
 
-        gather_keys(1)
-        score_pass(1)
+        for a in range(PASSES):
+            gather_keys(a)
+            score_pass(a)
 
         bias_less_q = keep.tile([P, ROW_TILES, I], F32, name="bias_less_q", tag="ky_tab%d" % (PASSES - 1))
-        for h in range(ROW_TILES):
-            nc.vector.tensor_tensor(bias_less_q[:, h, :], bias_row[:], q_ps[:, h, :], ALU.subtract)
+        nc.vector.tensor_tensor(
+            bias_less_q[:], bias_row[:].unsqueeze(1).to_broadcast([P, ROW_TILES, I]), q_ps[:], ALU.subtract
+        )
         for h in range(ROW_TILES):
             nc.vector.tensor_tensor(gap[:, h, :], a_ps[h][:], bias_less_q[:, h, :], ALU.add)
         for h in range(ROW_TILES):

@@ -25,6 +25,11 @@ PLANES = PASSES * PACK
 PAD = 8
 ROW_TILES = J // P
 PAIRS = 3
+LIST_ROWS = 16
+QUADRANT = 32
+BLOCK_PARTS = 8
+CX_SLOT, WC_SLOT = PASSES, PASSES + 1
+RUN = 4
 
 
 def tile_list_scores_steps_listed_tworank_kernel(
@@ -35,8 +40,8 @@ def tile_list_scores_steps_listed_tworank_kernel(
         keep = ctx.enter_context(tc.tile_pool(name="keep", bufs=1))
         psum = ctx.enter_context(tc.psum_pool(name="psum", bufs=1))
 
-        tok_list = keep.tile([P, J // 16], U16, name="tok_list")
-        key_list = keep.tile([P, I // 16], U16, name="key_list")
+        tok_list = keep.tile([P, J // LIST_ROWS], U16, name="tok_list")
+        key_list = keep.tile([P, I // LIST_ROWS], U16, name="key_list")
         x_pairs = [keep.tile([P, 2, T], F32, name="x_pair%d" % n) for n in range(PAIRS)]
         x_last = [keep.tile([P, T], F32, name="x_last%d" % n) for n in range(2)]
         x_rows = [x_pairs[n][:, e, :] for n in range(PAIRS) for e in range(2)] + [x_last[0][:], x_last[1][:]]
@@ -44,7 +49,7 @@ def tile_list_scores_steps_listed_tworank_kernel(
         ky_sc_tab = keep.tile([P, PASSES, V], U8, name="ky_sc_tab")
         cx_codes = keep.tile([P, 2 * J], U8, name="cx_codes", align_bytes=64)
         wc_codes = keep.tile([P, I], U32, name="wc_codes", align_bytes=64)
-        scales = keep.tile([P, 4, J], U8, name="scales", align_bytes=64)
+        scales = keep.tile([P, WC_SLOT + 1, J], U8, name="scales", align_bytes=64)
         factor = keep.tile([P, PASSES, PACK], F32, name="factor")
         bias_col = keep.tile([P, 2], F32, name="bias_col")
         bias_row = keep.tile([P, I], F32, name="bias_row")
@@ -70,13 +75,18 @@ def tile_list_scores_steps_listed_tworank_kernel(
 
         zeros = keep.tile([P, PLANES], F32, name="zeros")
         nc.gpsimd.memset(ky_sc_tab[:].rearrange("p a v -> p (a v)").bitcast(I32), 0)
-        nc.gpsimd.memset(scales[:, 2:4, :].rearrange("p a v -> p (a v)").bitcast(I32), 0)
+        nc.gpsimd.memset(scales[:, CX_SLOT : WC_SLOT + 1, :].rearrange("p a v -> p (a v)").bitcast(I32), 0)
         nc.gpsimd.memset(zeros[:], 0.0)
         make_identity(nc, ident[:])
 
-        nc.scalar.dma_start(ky_sc_tab[0:P:8, :, :].bitcast(I32), ky_scales.bitcast(I32).rearrange("a q v -> q a v"))
-        nc.scalar.dma_start(scales[0:P:8, 2, :].bitcast(I32), cx_scales.bitcast(I32)[0])
-        nc.scalar.dma_start(scales[0:P:8, 3, :].bitcast(I32), wc_scales.bitcast(I32)[0])
+        nc.scalar.dma_start(factor[:], fk.rearrange("(a p t) o -> p a (t o)", a=PASSES, t=PACK))
+        nc.scalar.dma_start(bias_col[:], bi.rearrange("o (p e) -> p (o e)", e=2))
+
+        nc.scalar.dma_start(
+            ky_sc_tab[0:P:BLOCK_PARTS, :, :].bitcast(I32), ky_scales.bitcast(I32).rearrange("a q v -> q a v")
+        )
+        nc.scalar.dma_start(scales[0:P:BLOCK_PARTS, CX_SLOT, :].bitcast(I32), cx_scales.bitcast(I32)[0])
+        nc.scalar.dma_start(scales[0:P:BLOCK_PARTS, WC_SLOT, :].bitcast(I32), wc_scales.bitcast(I32)[0])
         nc.scalar.activation(lined[:, :, PAD - 1], zeros[:], COPY)
 
         def load_pair(n):
@@ -86,27 +96,29 @@ def tile_list_scores_steps_listed_tworank_kernel(
         nc.sync.dma_start(key_list[:], offs2)
         load_pair(0)
         nc.sync.dma_start(tok_list[:], offs)
-        nc.sync.dma_start(factor[:], fk.rearrange("(a p t) o -> p a (t o)", a=PASSES, t=PACK))
-        nc.sync.dma_start(bias_col[:], bi.rearrange("o (p e) -> p (o e)", e=2))
         load_pair(1)
         load_pair(2)
-        nc.sync.dma_start(x_last[0][:], xv[PASSES - 1, :, 2, :])
+        for n in range(2):
+            nc.sync.dma_start(x_last[n][:], xv[PASSES - 1, :, PACK - 2 + n, :])
 
         for a in range(PASSES):
             nc.vector.tensor_copy(ky_sc[:, a, :], ky_sc_tab[:, a, :].indirect(key_list[:]))
         nc.vector.tensor_copy(
-            scales[:, 0:2, :].rearrange("p a v -> p (a v)").bitcast(I32),
+            scales[:, 0:PASSES, :].rearrange("p a v -> p (a v)").bitcast(I32),
             ky_sc[:].rearrange("p a v -> p (a v)").bitcast(I32),
         )
         scale_words = scales[:].rearrange("p a v -> p (a v)").bitcast(I32)
-        for r in range(1, 4):
-            nc.sync.dma_start(scale_words[r:P:32, :], scale_words[8 * r : P : 32, :])
+        for r in range(1, QUADRANT // BLOCK_PARTS):
+            nc.sync.dma_start(scale_words[r:P:QUADRANT, :], scale_words[BLOCK_PARTS * r : P : QUADRANT, :])
 
-        nc.sync.dma_start(x_last[1][:], xv[PASSES - 1, :, 3, :])
         nc.sync.dma_start(wc_codes[:].bitcast(I32), wc_words[0].rearrange("p n t -> p (n t)").bitcast(I32))
         nc.sync.dma_start(cx_codes[:].bitcast(I32), cx_words[0].bitcast(I32))
         for a in range(PASSES):
             nc.sync.dma_start(ky_tab[a][:].bitcast(I32), ky_words[a].rearrange("p n t -> p (n t)").bitcast(I32))
+
+        def gather_tokens(dst, plane, first, count):
+            entries = tok_list[:, first // LIST_ROWS : (first + count) // LIST_ROWS]
+            nc.scalar.activation(dst, x_rows[plane].indirect(entries), COPY)
 
         def take_step(dst, plane, first, count):
             nc.vector.scalar_tensor_tensor(
@@ -114,9 +126,6 @@ def tile_list_scores_steps_listed_tworank_kernel(
                 lined[:, plane, PAD - 1 + first : PAD - 1 + first + count], -0.6,
                 lined[:, plane, PAD + first : PAD + first + count], ALU.mult, ALU.add,
             )
-
-        def gather_tokens(dst, plane, first, count):
-            nc.scalar.activation(dst, x_rows[plane].indirect(tok_list[:, first // 16 : (first + count) // 16]), COPY)
 
         def factor_of(plane):
             a, t = divmod(plane, PACK)
@@ -135,8 +144,8 @@ def tile_list_scores_steps_listed_tworank_kernel(
 
         def weave(a, first, count):
             nc.vector.tensor_copy(
-                u_bf[a][:, first : first + count, :].rearrange("p (c i) t -> p c t i", i=4),
-                flat[:, a * PACK : (a + 1) * PACK, first : first + count].rearrange("p t (c i) -> p c t i", i=4),
+                u_bf[a][:, first : first + count, :].rearrange("p (c i) t -> p c t i", i=RUN),
+                flat[:, a * PACK : (a + 1) * PACK, first : first + count].rearrange("p t (c i) -> p c t i", i=RUN),
             )
 
         def quantize(a, first, count):
@@ -145,30 +154,16 @@ def tile_list_scores_steps_listed_tworank_kernel(
                 in_=u_bf[a][:, first : first + count, :].rearrange("p j t -> p (j t)"),
             )
 
-        def gather_keys(a):
-            nc.vector.tensor_copy(ky_codes[a][:], ky_tab[a][:].indirect(key_list[:]))
-
-        def score_pass(a):
-            for h in range(ROW_TILES):
-                rows = slice(h * P, (h + 1) * P)
-                nc.tensor.matmul_mx(
-                    out=a_ps[h][:],
-                    lhsT=u_codes[a][:, rows].bitcast(E5M2X4), lhsT_scale=u_sc[a][:, rows],
-                    rhs=ky_codes[a][:].bitcast(E5M2X4), rhs_scale=scales[:, a, :],
-                    start=(a == 0), stop=(a == PASSES - 1),
-                )
-
         for e in range(2):
             nc.tensor.transpose(bias_ps[:, e, :], bias_col[:, e : e + 1].to_broadcast([P, P]), ident[:])
         nc.scalar.copy(bias_row[:].rearrange("m (p e) -> m p e", e=2), bias_ps[:].rearrange("m e p -> m p e"))
 
-        for even in (0, 2):
+        for even in range(0, PACK, 2):
             gather_tokens(work[:, even, :], even, 0, J)
             gather_tokens(lined[:, even + 1, PAD:], even + 1, 0, J)
             factor_then_step(even, 0, J)
             step_then_factor(even + 1)
         weave(0, 0, J)
-
         quantize(0, 0, J)
 
         for plane in range(PACK, PLANES - 1):
@@ -188,15 +183,22 @@ def tile_list_scores_steps_listed_tworank_kernel(
             nc.tensor.matmul_mx(
                 out=q_ps[:, h, :],
                 lhsT=cx_codes[:, 2 * h * P : 2 * (h + 1) * P].bitcast(E2M1X4),
-                lhsT_scale=scales[:, 2, h * P : (h + 1) * P],
-                rhs=wc_codes[:].bitcast(E4M3X4), rhs_scale=scales[:, 3, :],
+                lhsT_scale=scales[:, CX_SLOT, h * P : (h + 1) * P],
+                rhs=wc_codes[:].bitcast(E4M3X4), rhs_scale=scales[:, WC_SLOT, :],
                 start=True, stop=True,
             )
         nc.scalar.activation(half_q[:], q_ps[:], COPY, scale=0.5)
 
         for a in range(PASSES):
-            gather_keys(a)
-            score_pass(a)
+            nc.vector.tensor_copy(ky_codes[a][:], ky_tab[a][:].indirect(key_list[:]))
+            for h in range(ROW_TILES):
+                rows = slice(h * P, (h + 1) * P)
+                nc.tensor.matmul_mx(
+                    out=a_ps[h][:],
+                    lhsT=u_codes[a][:, rows].bitcast(E5M2X4), lhsT_scale=u_sc[a][:, rows],
+                    rhs=ky_codes[a][:].bitcast(E5M2X4), rhs_scale=scales[:, a, :],
+                    start=(a == 0), stop=(a == PASSES - 1),
+                )
 
         bias_less_q = keep.tile([P, ROW_TILES, I], F32, name="bias_less_q", tag="ky_tab%d" % (PASSES - 1))
         nc.vector.tensor_tensor(

from contextlib import ExitStack

import concourse.mybir as mybir
from concourse.masks import make_identity

K, T, J, I, V, L = 1024, 1024, 256, 256, 1024, 512
FLOPS = 2 * J * I * (K + L)

F32 = mybir.dt.float32
BF16 = mybir.dt.bfloat16
I32 = mybir.dt.int32
U32 = mybir.dt.uint32
U16 = mybir.dt.uint16
U8 = mybir.dt.uint8
E5M2X4 = mybir.dt.float8_e5m2_x4
E4M3X4 = mybir.dt.float8_e4m3fn_x4
E2M1X4 = mybir.dt.float4_e2m1fn_x4
ALU = mybir.AluOpType
COPY = mybir.ActivationFunctionType.Copy

P = 128
PACK = 4
PASSES = K // (P * PACK)
PLANES = PASSES * PACK
PAD = 8
ROW_TILES = J // P
PAIRS = 3
LIST_ROWS = 16
QUADRANT = 32
BLOCK_PARTS = 8
CX_SLOT, WC_SLOT = PASSES, PASSES + 1
RUN = 4


def tile_list_scores_steps_listed_tworank_kernel(
    tc, xf, fk, ky_words, ky_scales, bi, cx_words, cx_scales, wc_words, wc_scales, offs, offs2, out
):
    nc = tc.nc
    with ExitStack() as ctx:
        keep = ctx.enter_context(tc.tile_pool(name="keep", bufs=1))
        psum = ctx.enter_context(tc.psum_pool(name="psum", bufs=1))

        tok_list = keep.tile([P, J // LIST_ROWS], U16, name="tok_list")
        key_list = keep.tile([P, I // LIST_ROWS], U16, name="key_list")
        x_pairs = [keep.tile([P, 2, T], F32, name="x_pair%d" % n) for n in range(PAIRS)]
        x_last = [keep.tile([P, T], F32, name="x_last%d" % n) for n in range(2)]
        x_rows = [x_pairs[n][:, e, :] for n in range(PAIRS) for e in range(2)] + [x_last[0][:], x_last[1][:]]
        ky_tab = [keep.tile([P, V], U32, name="ky_tab%d" % a, tag="ky_tab%d" % a) for a in range(PASSES)]
        ky_sc_tab = keep.tile([P, PASSES, V], U8, name="ky_sc_tab")
        cx_codes = keep.tile([P, 2 * J], U8, name="cx_codes", align_bytes=64)
        wc_codes = keep.tile([P, I], U32, name="wc_codes", align_bytes=64)
        scales = keep.tile([P, WC_SLOT + 1, J], U8, name="scales", align_bytes=64)
        factor = keep.tile([P, PASSES, PACK], F32, name="factor")
        bias_col = keep.tile([P, 2], F32, name="bias_col")
        bias_row = keep.tile([P, I], F32, name="bias_row")
        ident = keep.tile([P, P], F32, name="ident")
        work = keep.tile([P, PLANES, J], F32, name="work")
        lined = keep.tile([P, PLANES, PAD + J], F32, name="lined")
        flat = keep.tile([P, PLANES, J], BF16, name="flat")
        u_bf = [keep.tile([P, J, PACK], BF16, name="u_bf%d" % a, align_bytes=64) for a in range(PASSES)]
        u_codes = [keep.tile([P, J], U32, name="u_codes%d" % a, align_bytes=64) for a in range(PASSES)]
        u_sc = [keep.tile([P, J], U8, name="u_sc%d" % a, align_bytes=64) for a in range(PASSES)]
        ky_codes = [keep.tile([P, I], U32, name="ky_codes%d" % a, align_bytes=64) for a in range(PASSES)]
        ky_sc = keep.tile([P, PASSES, I], U8, name="ky_sc")
        half_q = keep.tile([P, ROW_TILES, I], F32, name="half_q")
        gap = keep.tile([P, ROW_TILES, I], F32, name="gap")
        bent = keep.tile([P, ROW_TILES, I], F32, name="bent")
        res = keep.tile([P, ROW_TILES, I], F32, name="res")

        bias_ps = psum.tile([P, 2, P], F32, name="bias_ps")
        q_ps = psum.tile([P, ROW_TILES, I], F32, name="q_ps")
        a_ps = [psum.tile([P, I], F32, name="a_ps%d" % h) for h in range(ROW_TILES)]

        xv = xf.rearrange("(a p t) n -> a p t n", a=PASSES, t=PACK)

        zeros = keep.tile([P, PLANES], F32, name="zeros")
        nc.gpsimd.memset(ky_sc_tab[:].rearrange("p a v -> p (a v)").bitcast(I32), 0)
        nc.gpsimd.memset(scales[:, CX_SLOT : WC_SLOT + 1, :].rearrange("p a v -> p (a v)").bitcast(I32), 0)
        nc.gpsimd.memset(zeros[:], 0.0)
        make_identity(nc, ident[:])

        nc.scalar.dma_start(factor[:], fk.rearrange("(a p t) o -> p a (t o)", a=PASSES, t=PACK))
        nc.scalar.dma_start(bias_col[:], bi.rearrange("o (p e) -> p (o e)", e=2))

        nc.scalar.dma_start(
            ky_sc_tab[0:P:BLOCK_PARTS, :, :].bitcast(I32), ky_scales.bitcast(I32).rearrange("a q v -> q a v")
        )
        nc.scalar.dma_start(scales[0:P:BLOCK_PARTS, CX_SLOT, :].bitcast(I32), cx_scales.bitcast(I32)[0])
        nc.scalar.dma_start(scales[0:P:BLOCK_PARTS, WC_SLOT, :].bitcast(I32), wc_scales.bitcast(I32)[0])
        nc.scalar.activation(lined[:, :, PAD - 1], zeros[:], COPY)

        def load_pair(n):
            a, t = divmod(2 * n, PACK)
            nc.sync.dma_start(x_pairs[n][:], xv[a, :, t : t + 2, :])

        nc.sync.dma_start(key_list[:], offs2)
        load_pair(0)
        nc.sync.dma_start(tok_list[:], offs)
        load_pair(1)
        load_pair(2)
        for n in range(2):
            nc.sync.dma_start(x_last[n][:], xv[PASSES - 1, :, PACK - 2 + n, :])

        for a in range(PASSES):
            nc.vector.tensor_copy(ky_sc[:, a, :], ky_sc_tab[:, a, :].indirect(key_list[:]))
        nc.vector.tensor_copy(
            scales[:, 0:PASSES, :].rearrange("p a v -> p (a v)").bitcast(I32),
            ky_sc[:].rearrange("p a v -> p (a v)").bitcast(I32),
        )
        scale_words = scales[:].rearrange("p a v -> p (a v)").bitcast(I32)
        for r in range(1, QUADRANT // BLOCK_PARTS):
            nc.sync.dma_start(scale_words[r:P:QUADRANT, :], scale_words[BLOCK_PARTS * r : P : QUADRANT, :])

        nc.sync.dma_start(wc_codes[:].bitcast(I32), wc_words[0].rearrange("p n t -> p (n t)").bitcast(I32))
        nc.sync.dma_start(cx_codes[:].bitcast(I32), cx_words[0].bitcast(I32))
        for a in range(PASSES):
            nc.sync.dma_start(ky_tab[a][:].bitcast(I32), ky_words[a].rearrange("p n t -> p (n t)").bitcast(I32))

        def gather_tokens(dst, plane, first, count):
            entries = tok_list[:, first // LIST_ROWS : (first + count) // LIST_ROWS]
            nc.scalar.activation(dst, x_rows[plane].indirect(entries), COPY)

        def take_step(dst, plane, first, count):
            nc.vector.scalar_tensor_tensor(
                dst[:, plane, first : first + count],
                lined[:, plane, PAD - 1 + first : PAD - 1 + first + count], -0.6,
                lined[:, plane, PAD + first : PAD + first + count], ALU.mult, ALU.add,
            )

        def factor_of(plane):
            a, t = divmod(plane, PACK)
            return factor[:, a, t : t + 1]

        def factor_then_step(plane, first, count):
            nc.scalar.activation(
                lined[:, plane, PAD + first : PAD + first + count], work[:, plane, first : first + count],
                COPY, scale=factor_of(plane),
            )
            take_step(flat, plane, first, count)

        def step_then_factor(plane):
            take_step(work, plane, 0, J)
            nc.vector.tensor_scalar(flat[:, plane, :], work[:, plane, :], factor_of(plane), None, ALU.mult)

        def weave(a, first, count):
            nc.vector.tensor_copy(
                u_bf[a][:, first : first + count, :].rearrange("p (c i) t -> p c t i", i=RUN),
                flat[:, a * PACK : (a + 1) * PACK, first : first + count].rearrange("p t (c i) -> p c t i", i=RUN),
            )

        def quantize(a, first, count):
            nc.vector.quantize_mx(
                out=u_codes[a][:, first : first + count].bitcast(E5M2X4), scales=u_sc[a][:, first : first + count],
                in_=u_bf[a][:, first : first + count, :].rearrange("p j t -> p (j t)"),
            )

        for e in range(2):
            nc.tensor.transpose(bias_ps[:, e, :], bias_col[:, e : e + 1].to_broadcast([P, P]), ident[:])
        nc.scalar.copy(bias_row[:].rearrange("m (p e) -> m p e", e=2), bias_ps[:].rearrange("m e p -> m p e"))

        for even in range(0, PACK, 2):
            gather_tokens(work[:, even, :], even, 0, J)
            gather_tokens(lined[:, even + 1, PAD:], even + 1, 0, J)
            factor_then_step(even, 0, J)
            step_then_factor(even + 1)
        weave(0, 0, J)
        quantize(0, 0, J)

        for plane in range(PACK, PLANES - 1):
            gather_tokens(lined[:, plane, PAD:], plane, 0, J)
        for plane in range(PACK, PLANES - 1):
            step_then_factor(plane)
        for h in range(ROW_TILES):
            gather_tokens(work[:, PLANES - 1, h * P : (h + 1) * P], PLANES - 1, h * P, P)
        for h in range(ROW_TILES):
            factor_then_step(PLANES - 1, h * P, P)
        for h in range(ROW_TILES):
            weave(1, h * P, P)
        for h in range(ROW_TILES):
            quantize(1, h * P, P)

        for h in range(ROW_TILES):
            nc.tensor.matmul_mx(
                out=q_ps[:, h, :],
                lhsT=cx_codes[:, 2 * h * P : 2 * (h + 1) * P].bitcast(E2M1X4),
                lhsT_scale=scales[:, CX_SLOT, h * P : (h + 1) * P],
                rhs=wc_codes[:].bitcast(E4M3X4), rhs_scale=scales[:, WC_SLOT, :],
                start=True, stop=True,
            )
        nc.scalar.activation(half_q[:], q_ps[:], COPY, scale=0.5)

        for a in range(PASSES):
            nc.vector.tensor_copy(ky_codes[a][:], ky_tab[a][:].indirect(key_list[:]))
            for h in range(ROW_TILES):
                rows = slice(h * P, (h + 1) * P)
                nc.tensor.matmul_mx(
                    out=a_ps[h][:],
                    lhsT=u_codes[a][:, rows].bitcast(E5M2X4), lhsT_scale=u_sc[a][:, rows],
                    rhs=ky_codes[a][:].bitcast(E5M2X4), rhs_scale=scales[:, a, :],
                    start=(a == 0), stop=(a == PASSES - 1),
                )

        bias_less_q = keep.tile([P, ROW_TILES, I], F32, name="bias_less_q", tag="ky_tab%d" % (PASSES - 1))
        nc.vector.tensor_tensor(
            bias_less_q[:], bias_row[:].unsqueeze(1).to_broadcast([P, ROW_TILES, I]), q_ps[:], ALU.subtract
        )
        for h in range(ROW_TILES):
            nc.vector.tensor_tensor(gap[:, h, :], a_ps[h][:], bias_less_q[:, h, :], ALU.add)
        for h in range(ROW_TILES):
            nc.vector.scalar_tensor_tensor(bent[:, h, :], gap[:, h, :], -0.5, gap[:, h, :], ALU.mult, ALU.max)
        for h in range(ROW_TILES):
            nc.vector.tensor_tensor(res[:, h, :], bent[:, h, :], half_q[:, h, :], ALU.add)
            nc.sync.dma_start(out[h * P : (h + 1) * P, :], res[:, h, :])
